import numpy as np
import ml_dtypes


def mxq(x, axis, fmt="e4m3"):
    dtype, down = {"e4m3": (ml_dtypes.float8_e4m3fn, 7), "e5m2": (ml_dtypes.float8_e5m2, 14)}[fmt]
    v = np.moveaxis(np.asarray(x, np.float32).astype(ml_dtypes.bfloat16).astype(np.float64), axis, -1)
    blocks = v.reshape(v.shape[:-1] + (-1, 32))
    amax = np.abs(blocks).max(-1, keepdims=True)
    byte = np.maximum(np.where(amax > 0, np.frexp(amax)[1] - 1 + 127, 0) - down, 1)
    scale = np.exp2(byte - 127.0)
    codes = (blocks / scale).astype(np.float32).astype(dtype).astype(np.float64)
    return np.moveaxis((codes * scale).reshape(v.shape), -1, axis)


WIDE = False


def mx_kscale(k):
    if not WIDE:
        return np.ones(k)
    levels = np.array([10, -10, 5, -5, 0])
    if k % 512:
        return np.exp2(np.random.permutation(np.resize(levels, k // 32))).repeat(32)
    a = np.empty((k // 512, 16))
    for p in range(k // 512):
        a[p, :8] = np.random.permutation(np.resize(levels, 8))
        for g in range(8):
            far = levels[np.abs(levels - a[p, g]) >= 10]
            a[p, g + 8] = far[np.random.randint(len(far))]
    return np.exp2(a.ravel()).repeat(32)


def f64(x):
    return np.asarray(x).astype(np.float64)


def striped(idx):
    return np.tile(idx.reshape(-1, 16).T, (8, 1)).astype(np.uint16)


def unstriped(offs):
    return offs[:16].T.reshape(-1).astype(np.int64)


E2M1 = np.array([0.0, 0.5, 1.0, 1.5, 2.0, 3.0, 4.0, 6.0, -0.0, -0.5, -1.0, -1.5, -2.0, -3.0, -4.0, -6.0])


def pack_weight(w, fmt):
    k, n = w.shape
    w = f64(np.asarray(w, np.float32).astype(ml_dtypes.bfloat16)).reshape(k // 32, 32, n)
    amax = np.abs(w).max(1)
    if fmt == "e4m3":
        byte = np.frexp(amax)[1] - 1 + 127 - 7
    else:
        mant, ex = np.frexp(amax / 6.0)
        byte = np.where(mant > 0.5, ex, ex - 1) + 127
    byte = np.clip(np.where(amax > 0, byte, 1), 1, 254)
    scaled = (w * np.exp2(127.0 - byte)[:, None, :]).reshape(k, n).astype(np.float32)
    by_word = np.ascontiguousarray(scaled.reshape(k // 512, 128, 4, n).transpose(0, 1, 3, 2))
    if fmt == "e4m3":
        words = by_word.astype(ml_dtypes.float8_e4m3fn).view(np.uint8)
    else:
        c = by_word.astype(ml_dtypes.float4_e2m1fn).view(np.uint8) & 0xF
        words = (c[..., 0::2] | (c[..., 1::2] << 4)).reshape(k // 512, 128, 2 * n)
    return np.ascontiguousarray(words), np.ascontiguousarray(byte.astype(np.uint8).reshape(k // 512, 16, n))


def unpack_weight(words, scales, fmt):
    g, _, n = scales.shape
    words = np.ascontiguousarray(words).reshape(g, 128, n, -1)
    if fmt == "e4m3":
        vals = words.view(ml_dtypes.float8_e4m3fn).astype(np.float64)
    else:
        nib = np.empty((g, 128, n, 4), np.uint8)
        nib[..., 0::2] = words & 0xF
        nib[..., 1::2] = words >> 4
        vals = E2M1[nib]
    vals = vals * np.repeat(np.exp2(scales.astype(np.float64) - 127.0), 8, axis=1)[..., None]
    return vals.transpose(0, 1, 3, 2).reshape(g * 512, n)


def gelu(v):
    return 0.5 * v * (1.0 + np.tanh(np.sqrt(2.0 / np.pi) * (v + 0.044715 * v**3)))


K, T, S, H, T2, P, N = 1024, 4096, 1024, 512, 2048, 1024, 512

def setup_inputs():
    n = np.random.standard_normal
    s = mx_kscale(K)[:, None]
    u = mx_kscale(H)[:, None]
    d = {}
    d["tab_words"], d["tab_scales"] = pack_weight(n((K, T)) * s, "e4m3")
    d["offs"] = striped(np.random.permutation(T)[:S])
    d["w1"] = (n((K, H)) / s / K ** 0.5).astype(np.float32)
    d["w2_words"], d["w2_scales"] = pack_weight(n((K, H)) / s / K ** 0.5, "e2m1")
    d["w3_words"], d["w3_scales"] = pack_weight(n((K, H)) / s / K ** 0.5, "e4m3")
    d["gain"] = (np.exp(0.3 * n(H)) * u[:, 0]).astype(np.float32)
    d["page0"] = (n((H, T2)) * u).astype(np.float32)
    d["wgs"] = np.exp(0.3 * n((128, S))).astype(np.float32)
    d["offs2"] = striped(np.random.permutation(T2)[:S])
    d["offs3"] = striped(np.random.permutation(T2)[:P])
    d["mid"] = ((0.6 + 0.5 * n(H)) * u[:, 0]).astype(np.float32)
    d["w4"] = (1.2 * n((H, N)) / u / H ** 0.5).astype(np.float32)
    d["page1"] = n((N, T2)).astype(np.float32)
    d["wgo"] = np.exp(0.3 * n((128, P))).astype(np.float32)
    d["offs4"] = striped(np.random.permutation(T2)[:P])
    return d

def reference(tab_words, tab_scales, offs, w1, w2_words, w2_scales, w3_words, w3_scales, gain,
              page0, wgs, offs2, offs3, mid, w4, page1, wgo, offs4):
    v = unpack_weight(tab_words, tab_scales, "e4m3")[:, unstriped(offs)]
    a = mxq(f64(w1), 0, "e4m3").T @ v
    b = unpack_weight(w2_words, w2_scales, "e2m1").T @ v
    e = unpack_weight(w3_words, w3_scales, "e4m3").T @ v
    h = (np.maximum(a, b) - np.minimum(a, e)) * f64(gain)[:, None]
    page = f64(page0).copy()
    page[:, unstriped(offs2)] = np.tile(f64(wgs), (H // 128, 1)) * h
    x = page[:, unstriped(offs3)] - f64(mid)[:, None]
    y = mxq(f64(w4), 0, "e4m3").T @ mxq(x, 0, "e4m3")
    y = 0.5 * y * (1.0 + np.tanh(0.7978845608 * (y + 0.044715 * y ** 3)))
    out = f64(page1).copy()
    out[:, unstriped(offs4)] = np.tile(f64(wgo), (N // 128, 1)) * y
    return out

@@ -1,0 +1,353 @@
+from contextlib import ExitStack
+
+import concourse.mybir as mybir
+from concourse.masks import make_identity
+
+K, T, S, H, T2, NP, N = 1024, 4096, 1024, 512, 2048, 1024, 512
+FLOPS = 3 * 2 * K * H * S + 2 * H * N * NP
+
+F32 = mybir.dt.float32
+BF16 = mybir.dt.bfloat16
+I32 = mybir.dt.int32
+U32 = mybir.dt.uint32
+U16 = mybir.dt.uint16
+U8 = mybir.dt.uint8
+FP8X4 = mybir.dt.float8_e4m3fn_x4
+FP4X4 = mybir.dt.float4_e2m1fn_x4
+ALU = mybir.AluOpType
+ACT = mybir.ActivationFunctionType
+
+P = 128
+HALF = 512
+WHOLE = 2
+PATHS = ["3V","1V","1V","1V","1V","1V","1V","1V"]
+
+
+def tile_list_address_repair_page_kernel(
+    tc, tab_words, tab_scales, offs, w1, w2_words, w2_scales, w3_words, w3_scales, gain,
+    page0, wgs, offs2, offs3, mid, w4, page1, wgo, offs4, out,
+):
+    nc = tc.nc
+    with ExitStack() as ctx:
+        lists = ctx.enter_context(tc.tile_pool(name="lists", bufs=1))
+        sb = ctx.enter_context(tc.tile_pool(name="sb", bufs=1))
+        psum = ctx.enter_context(tc.psum_pool(name="psum", bufs=1))
+
+        def sbuf(shape, dtype, name, tag=None, bufs=1):
+            return sb.tile(shape, dtype, name=name, tag=tag or name, bufs=bufs, align_bytes=64)
+
+        def bank(i, shape, name):
+            return psum.tile(shape, F32, name=name, tag="bank%d" % i)
+
+        def load_list(src, name):
+            t = lists.tile([P, 64], U16, name=name)
+            nc.sync.dma_start(t[:], src)
+            return t
+
+        def half_of(lst, h):
+            return lst[:, 32 * h : 32 * h + 32]
+
+        tab_sc = sbuf([P, T], U8, "tab_sc")
+        nc.vector.memset(tab_sc[:].bitcast(I32), 0)
+        w3_sc = sbuf([P, 2, H], U8, "w3_sc")
+        nc.vector.memset(w3_sc[:].rearrange("p a n -> p (a n)").bitcast(I32), 0)
+        w2_sc = sbuf([P, 2, H], U8, "w2_sc")
+        nc.gpsimd.memset(w2_sc[:].rearrange("p a n -> p (a n)").bitcast(I32), 0)
+        v_sc1 = sbuf([P, S], U8, "v_sc1")
+        nc.vector.memset(v_sc1[:].bitcast(I32), 0)
+        warm = sbuf([P, 2], F32, "warm")
+        nc.vector.memset(warm[:, 0:1], 0.0)
+        nc.scalar.activation(warm[:, 1:2], warm[:, 0:1], ACT.Gelu_apprx_tanh)
+
+        ident = sbuf([P, P], F32, "ident")
+        make_identity(nc, ident[:])
+
+        def load_w1(c0, c1, tag):
+            t = sbuf([P, 2, 4, P * (c1 - c0)], F32, "w1_raw%d" % c0, tag=tag)
+            for a in range(2):
+                rows = w1[512 * a : 512 * (a + 1), P * c0 : P * c1]
+                nc.sync.dma_start(t[:, a, :, :], rows.rearrange("(p j) c -> p j c", j=4))
+            return t
+
+        def load_w23(c0, c1):
+            t2 = sbuf([P, 2, 2 * P * (c1 - c0)], U8, "w2_w%d" % c0)
+            src2 = w2_words.rearrange("a p n -> p a n")[:, :, 2 * P * c0 : 2 * P * c1]
+            nc.sync.dma_start(t2[:].bitcast(I32), src2.bitcast(I32))
+            t3 = sbuf([P, 2, P * (c1 - c0)], U32, "w3_w%d" % c0)
+            src3 = w3_words.rearrange("a p n t -> p a (n t)")[:, :, 4 * P * c0 : 4 * P * c1]
+            nc.sync.dma_start(t3[:].bitcast(I32), src3.bitcast(I32))
+            return t2, t3
+
+        def load_tab(a):
+            t = sbuf([P, T], U32, "tab_w%d" % a, tag="tab%d" % a)
+            nc.sync.dma_start(t[:].bitcast(I32), tab_words[a].rearrange("p t i -> p (t i)").bitcast(I32))
+            return t
+
+        def load_rows(src, c, name, tag=None):
+            t = sbuf([P, T2], F32, name, tag=tag)
+            nc.sync.dma_start(t[:], src[P * c : P * (c + 1), :])
+            return t
+
+        def load_column(vec, name):
+            t = sbuf([P, 4], F32, name)
+            with nc.allow_non_contiguous_dma(reason="one value a partition"):
+                nc.sync.dma_start(t[:], vec.rearrange("(c p) -> p c", p=P))
+            return t
+
+        def load_half(src, h, name):
+            t = sbuf([P, HALF], F32, name)
+            nc.sync.dma_start(t[:], src[:, HALF * h : HALF * (h + 1)])
+            return t
+
+        idx = load_list(offs, "idx")
+        w1_raw0 = load_w1(0, 1, "w1_raw0")
+        for q in range(4):
+            nc.sync.dma_start(
+                tab_sc[32 * q : 32 * q + 8, :].bitcast(I32), tab_scales[:, 4 * q : 4 * q + 4, :].bitcast(I32)
+            )
+        tab0 = load_tab(0)
+        for plane, src, queue in ((w3_sc, w3_scales, nc.sync), (w2_sc, w2_scales, nc.gpsimd)):
+            for q in range(4):
+                queue.dma_start(
+                    plane[32 * q : 32 * q + 4, :, :].bitcast(I32),
+                    src[:, 4 * q : 4 * q + 4, :].rearrange("a r n -> r a n").bitcast(I32),
+                )
+        w2_0, w3_0 = load_w23(0, 1)
+        tab1 = load_tab(1)
+        wgs_t = sbuf([P, S], F32, "wgs_t")
+        nc.sync.dma_start(wgs_t[:, 0:HALF], wgs[:, 0:HALF])
+        pg0 = [load_rows(page0, 0, "page0_0")]
+        gain_t = load_column(gain, "gain_t")
+        idx2 = load_list(offs2, "idx2")
+        w1_raw1 = load_w1(1, 2, "w1_raw1")
+        w2_r, w3_r = load_w23(1, 4)
+        nc.sync.dma_start(wgs_t[:, HALF:S], wgs[:, HALF:S])
+        idx3 = load_list(offs3, "idx3")
+        pg0.append(load_rows(page0, 1, "page0_1"))
+        w1_raw2 = load_w1(2, 4, "w1_raw2")
+        pg0.append(load_rows(page0, 2, "page0_2"))
+        mid_t = load_column(mid, "mid_t")
+        pg0.append(load_rows(page0, 3, "page0_3"))
+
+        v_sc = sbuf([P, S], U8, "v_sc")
+        nc.vector.tensor_copy(v_sc[:], tab_sc[:].indirect(idx[:]))
+        for q in range(4):
+            nc.gpsimd.dma_start(
+                v_sc1[32 * q : 32 * q + 4, :].bitcast(I32), v_sc[32 * q + 4 : 32 * q + 8, :].bitcast(I32)
+            )
+
+        def quantize_w1(c):
+            raw, off = ((w1_raw0, 0), (w1_raw1, 0), (w1_raw2, 0), (w1_raw2, P))[c]
+            grouped = sbuf([P, 2, P, 4], BF16, "w1_bf%d" % c, tag="w1_bf", bufs=2)
+            nc.scalar.copy(grouped[:], raw[:, :, :, off : off + P].rearrange("p a j c -> p a c j"))
+            codes = sbuf([P, 2 * P], U32, "w1_q%d" % c, tag="wg_first" if c == 1 else "held%d" % c)
+            scales = sbuf([P, 2 * P], U8, "w1_s%d" % c)
+            nc.vector.quantize_mx(
+                out=codes[:].bitcast(FP8X4), scales=scales[:], in_=grouped[:].rearrange("p a c j -> p (a c j)")
+            )
+            return codes, scales
+
+        w1_q = {0: quantize_w1(0)}
+        v0 = sbuf([P, S], U32, "v0")
+        nc.vector.tensor_copy(v0[:], tab0[:].indirect(idx[:]))
+        v1 = []
+        for h in range(2):
+            t = sbuf([P, HALF], U32, "v1_%d" % h)
+            nc.vector.tensor_copy(t[:], tab1[:].indirect(half_of(idx, h)))
+            v1.append(t)
+
+        neg_gain = sbuf([P, 4], F32, "neg_gain")
+        nc.scalar.activation(neg_gain[:], gain_t[:], ACT.Copy, scale=-1.0)
+
+        def v_operand(which, a, h, j0, j1):
+            cols = slice(HALF * h + j0, HALF * h + j1)
+            if a == 0:
+                return v0[:, cols].bitcast(FP8X4), v_sc[:, cols]
+            plane = v_sc1[:, cols] if which == "b" else v_sc[4:P, cols]
+            return v1[h][:, j0:j1].bitcast(FP8X4), plane
+
+        def w_operand(which, a, c):
+            cols = slice(P * c, P * (c + 1))
+            if which == "a":
+                codes, scales = w1_q[c]
+                return codes[:, P * a : P * (a + 1)].bitcast(FP8X4), scales[:, P * a : P * (a + 1)]
+            k = 0 if c == 0 else c - 1
+            if which == "b":
+                t = w2_0 if c == 0 else w2_r
+                return t[:, a, 2 * P * k : 2 * P * (k + 1)].bitcast(FP4X4), w2_sc[:, a, cols]
+            t = w3_0 if c == 0 else w3_r
+            return t[:, a, P * k : P * (k + 1)].bitcast(FP8X4), w3_sc[:, a, cols]
+
+        ring = [0]
+
+        def next_bank(name):
+            ring[0] = ring[0] + 1
+            return bank((ring[0] - 1) % 3, [P, HALF], name)
+
+        def product_rows(which, c, h):
+            acc = next_bank("%s_%d_%d" % (which, c, h))
+            for a in range(2):
+                w, ws = w_operand(which, a, c)
+                v, vs = v_operand(which, a, h, 0, HALF)
+                nc.tensor.matmul_mx(out=acc[:], lhsT=w, lhsT_scale=ws, rhs=v, rhs_scale=vs, start=a == 0, stop=a == 1)
+            return acc
+
+        def product_turned(which, c, h):
+            acc = next_bank("%sT_%d_%d" % (which, c, h))
+            for jb in range(4):
+                for a in range(2):
+                    w, ws = w_operand(which, a, c)
+                    v, vs = v_operand(which, a, h, P * jb, P * (jb + 1))
+                    nc.tensor.matmul_mx(
+                        out=acc[:, P * jb : P * (jb + 1)], lhsT=v, lhsT_scale=vs, rhs=w, rhs_scale=ws,
+                        start=a == 0, stop=a == 1,
+                    )
+            return acc
+
+        def turn_and_add(acc, terms):
+            steps = [(b, term[b]) for term in terms for b in range(len(term))]
+            for i, (b, src) in enumerate(steps):
+                nc.tensor.matmul(
+                    acc[:, P * b : P * (b + 1)], src, ident[:], is_transpose=True,
+                    start=i == 0, stop=i == len(steps) - 1,
+                )
+
+        def blocks(t):
+            return [t[:, P * b : P * (b + 1)] for b in range(4)]
+
+        def work(name, u):
+            return sbuf([P, HALF], F32, "%s%d" % (name, u), tag=name, bufs=2)
+
+
+        def spread_3v(u, res):
+            c, h = divmod(u, 2)
+            pa = product_rows("a", c, h)
+            pe = product_rows("e", c, h)
+            pb = product_rows("b", c, h)
+            a_sb, hi = work("ta", u), work("tb", u)
+            lo = sbuf([P, HALF], F32, "lo%d" % u, tag="held%d" % u)
+            nc.scalar.copy(a_sb[:], pa[:])
+            nc.vector.tensor_tensor(lo[:], pe[:], a_sb[:], ALU.min)
+            nc.vector.tensor_tensor(hi[:], pb[:], a_sb[:], ALU.max)
+            nc.vector.tensor_tensor(res, lo[:], hi[:], ALU.subtract)
+
+        def spread_1v(u, res):
+            c, h = divmod(u, 2)
+            na, e_sb, b_sb = work("ta", u), work("te", u), work("tb", u)
+            pa = product_turned("a", c, h)
+            nc.scalar.activation(na[:], pa[:], ACT.Copy, scale=-1.0)
+            pb = product_turned("b", c, h)
+            nc.scalar.copy(b_sb[:], pb[:])
+            pe = product_turned("e", c, h)
+            nc.scalar.copy(e_sb[:], pe[:])
+            d1 = bank(3, [P, HALF], "d1_%d" % u)
+            turn_and_add(d1, [blocks(na), blocks(b_sb)])
+            d2 = bank(4 + u % 4, [P, HALF], "d2_%d" % u)
+            turn_and_add(d2, [blocks(na), blocks(e_sb)])
+            r1 = sbuf([P, HALF], F32, "r1_%d" % u, tag="held%d" % u)
+            nc.scalar.activation(r1[:], d1[:], ACT.Relu)
+            nc.vector.scalar_tensor_tensor(res, d2[:], 0.0, r1[:], ALU.min, ALU.subtract)
+
+        picked = {}
+
+        def pick_first(c, tag):
+            g = sbuf([P, HALF], F32, "g%d" % c, tag=tag)
+            nc.vector.tensor_copy(g[:], pg0[c][:].indirect(half_of(idx3, 0)))
+            picked[(c, 0)] = g[:]
+
+        for c in range(4):
+            if c == 3:
+                neg_h = sbuf([P, 4 * HALF], F32, "h_last", tag="late")
+            else:
+                neg_h = sbuf([P, S], F32, "h%d" % c, tag="h", bufs=2)
+            for h in range(2):
+                u = 2 * c + h
+                cols = slice(HALF * h, HALF * (h + 1))
+                if PATHS[u] == "3V":
+                    spread_3v(u, neg_h[:, cols])
+                else:
+                    spread_1v(u, neg_h[:, cols])
+                if c == 1:
+                    w1_q[u] = quantize_w1(u)
+                if c < WHOLE:
+                    if u == 0:
+                        wg = sbuf([P, HALF], F32, "wg_first")
+                    else:
+                        wg = sbuf([P, HALF], F32, "wg_half%d" % u)
+                    nc.scalar.activation(wg[:], wgs_t[:, cols], ACT.Copy, scale=neg_gain[:, c : c + 1])
+                    if h == 0 and c > 0:
+                        pick_first(c - 1, None)
+                    nc.vector.tensor_tensor(pg0[c][:].indirect(half_of(idx2, h)), neg_h[:, cols], wg[:], ALU.mult)
+                    if u == 0:
+                        w1_q[1] = quantize_w1(1)
+            if c >= WHOLE:
+                wg = sbuf([P, S], F32, "wg%d" % c)
+                nc.scalar.activation(wg[:], wgs_t[:], ACT.Copy, scale=neg_gain[:, c : c + 1])
+                pick_first(c - 1, "held%d" % (2 * c + 1))
+                nc.vector.tensor_tensor(pg0[c][:].indirect(idx2[:]), neg_h[:, 0:S], wg[:], ALU.mult)
+        pick_first(3, None)
+        late = sbuf([P, 4 * HALF], F32, "g_late", tag="late")
+        for c in range(4):
+            picked[(c, 1)] = late[:, HALF * c : HALF * (c + 1)]
+            nc.vector.tensor_copy(picked[(c, 1)], pg0[c][:].indirect(half_of(idx3, 1)))
+
+        w4_raw = sbuf([P, 4, N], F32, "w4_raw", tag="w1_raw2")
+        nc.sync.dma_start(w4_raw[:], w4.rearrange("(p j) n -> p j n", j=4))
+        idx4 = load_list(offs4, "idx4")
+        wgo_t = [load_half(wgo, h, "wgo%d" % h) for h in range(2)]
+        pg1 = [load_rows(page1, n, "page1_%d" % n, tag="tab%d" % n if n < 2 else None) for n in range(4)]
+        w4_bf = sbuf([P, N, 4], BF16, "w4_bf")
+        nc.scalar.copy(w4_bf[:], w4_raw[:].rearrange("p j n -> p n j"))
+        w4_q = sbuf([P, N], U32, "w4_q")
+        w4_s = sbuf([P, N], U8, "w4_s")
+        nc.vector.quantize_mx(out=w4_q[:].bitcast(FP8X4), scales=w4_s[:], in_=w4_bf[:].rearrange("p n j -> p (n j)"))
+        neg_mid = sbuf([P, 4], F32, "neg_mid")
+        nc.scalar.activation(neg_mid[:], mid_t[:], ACT.Copy, scale=-1.0)
+        mid_blocks = [neg_mid[:, c : c + 1].to_broadcast([P, P]) for c in range(4)]
+
+        def quantize_x(h, turn_banks, word_banks):
+            xi = sbuf([P, HALF, 2], F32, "xi%d" % h)
+            for pair in range(2):
+                words = bank(word_banks[pair], [P, 2, 2, P], "words%d_%d" % (h, pair))
+                for b in range(2):
+                    jb = 2 * pair + b
+                    xt = bank(turn_banks[jb], [P, H], "xt%d_%d" % (h, jb))
+                    turn_and_add(xt, [mid_blocks, [picked[(c, h)][:, P * jb : P * (jb + 1)] for c in range(4)]])
+                    xb = sbuf([P, 2, P, 2], BF16, "xb%d_%d" % (h, jb), tag="xb", bufs=4)
+                    nc.scalar.copy(xb[:], xt[:].rearrange("j (q u e) -> j u q e", u=2, e=2))
+                    xw = xb[:].rearrange("j u q e -> j (u q e)").bitcast(F32)
+                    for u in range(2):
+                        nc.tensor.transpose(words[:, b, u, :], xw[:, P * u : P * (u + 1)], ident[:])
+                nc.scalar.copy(
+                    xi[:, 2 * P * pair : 2 * P * (pair + 1), :].rearrange("p (b j) u -> p b j u", b=2),
+                    words[:].rearrange("p b u j -> p b j u"),
+                )
+            codes = sbuf([P, HALF], U32, "x_q%d" % h)
+            scales = sbuf([P, HALF], U8, "x_s%d" % h)
+            nc.vector.quantize_mx(
+                out=codes[:].bitcast(FP8X4), scales=scales[:],
+                in_=xi[:].rearrange("p j u -> p (j u)").bitcast(BF16),
+            )
+            return codes, scales
+
+        def put_result(n, h, x_q, y_bank):
+            y = bank(y_bank, [P, HALF], "y%d_%d" % (n, h))
+            cols = slice(P * n, P * (n + 1))
+            nc.tensor.matmul_mx(
+                out=y[:], lhsT=w4_q[:, cols].bitcast(FP8X4), lhsT_scale=w4_s[:, cols],
+                rhs=x_q[0][:].bitcast(FP8X4), rhs_scale=x_q[1][:], start=True, stop=True,
+            )
+            act = sbuf([P, HALF], F32, "act%d_%d" % (n, h), tag="act", bufs=3)
+            nc.scalar.activation(act[:], y[:], ACT.Gelu_apprx_tanh)
+            nc.vector.tensor_tensor(pg1[n][:].indirect(half_of(idx4, h)), act[:], wgo_t[h][:], ALU.mult)
+            if h == 1:
+                nc.sync.dma_start(out[P * n : P * (n + 1), :], pg1[n][:])
+
+        x0 = quantize_x(0, (0, 1, 2, 3), (4, 5))
+        put_result(0, 0, x0, 6)
+        put_result(1, 0, x0, 7)
+        x1 = quantize_x(1, (6, 7, 6, 7), (4, 5))
+        put_result(2, 0, x0, 4)
+        put_result(3, 0, x0, 5)
+        for n in range(4):
+            put_result(n, 1, x1, n)

@@ -101,7 +101,7 @@ def tile_list_address_repair_page_kernel(
 
         idx = load_list(offs, "idx")
         w1_raw0 = load_w1(0, 1, "w1_raw0")
-        for q in range(4):
+        for q in (0, 2, 1, 3):
             nc.sync.dma_start(
                 tab_sc[32 * q : 32 * q + 8, :].bitcast(I32), tab_scales[:, 4 * q : 4 * q + 4, :].bitcast(I32)
             )
@@ -114,6 +114,12 @@ def tile_list_address_repair_page_kernel(
                 )
         w2_0, w3_0 = load_w23(0, 1)
         tab1 = load_tab(1)
+        v_sc = sbuf([P, S], U8, "v_sc")
+        nc.vector.tensor_copy(v_sc[:], tab_sc[:].indirect(idx[:]))
+        for q in range(4):
+            nc.sync.dma_start(
+                v_sc1[32 * q : 32 * q + 4, :].bitcast(I32), v_sc[32 * q + 4 : 32 * q + 8, :].bitcast(I32)
+            )
         wgs_t = sbuf([P, S], F32, "wgs_t")
         nc.sync.dma_start(wgs_t[:, 0:HALF], wgs[:, 0:HALF])
         pg0 = [load_rows(page0, 0, "page0_0")]
@@ -129,25 +135,19 @@ def tile_list_address_repair_page_kernel(
         mid_t = load_column(mid, "mid_t")
         pg0.append(load_rows(page0, 3, "page0_3"))
 
-        v_sc = sbuf([P, S], U8, "v_sc")
-        nc.vector.tensor_copy(v_sc[:], tab_sc[:].indirect(idx[:]))
-        for q in range(4):
-            nc.gpsimd.dma_start(
-                v_sc1[32 * q : 32 * q + 4, :].bitcast(I32), v_sc[32 * q + 4 : 32 * q + 8, :].bitcast(I32)
-            )
 
-        def quantize_w1(c):
+        def quantize_w1(c, tag):
             raw, off = ((w1_raw0, 0), (w1_raw1, 0), (w1_raw2, 0), (w1_raw2, P))[c]
             grouped = sbuf([P, 2, P, 4], BF16, "w1_bf%d" % c, tag="w1_bf", bufs=2)
             nc.scalar.copy(grouped[:], raw[:, :, :, off : off + P].rearrange("p a j c -> p a c j"))
-            codes = sbuf([P, 2 * P], U32, "w1_q%d" % c, tag="wg_first" if c == 1 else "held%d" % c)
+            codes = sbuf([P, 2 * P], U32, "w1_q%d" % c, tag=tag)
             scales = sbuf([P, 2 * P], U8, "w1_s%d" % c)
             nc.vector.quantize_mx(
                 out=codes[:].bitcast(FP8X4), scales=scales[:], in_=grouped[:].rearrange("p a c j -> p (a c j)")
             )
             return codes, scales
 
-        w1_q = {0: quantize_w1(0)}
+        w1_q = {0: quantize_w1(0, None)}
         v0 = sbuf([P, S], U32, "v0")
         nc.vector.tensor_copy(v0[:], tab0[:].indirect(idx[:]))
         v1 = []
@@ -156,8 +156,6 @@ def tile_list_address_repair_page_kernel(
             nc.vector.tensor_copy(t[:], tab1[:].indirect(half_of(idx, h)))
             v1.append(t)
 
-        neg_gain = sbuf([P, 4], F32, "neg_gain")
-        nc.scalar.activation(neg_gain[:], gain_t[:], ACT.Copy, scale=-1.0)
 
         def v_operand(which, a, h, j0, j1):
             cols = slice(HALF * h + j0, HALF * h + j1)
@@ -178,14 +176,13 @@ def tile_list_address_repair_page_kernel(
             t = w3_0 if c == 0 else w3_r
             return t[:, a, P * k : P * (k + 1)].bitcast(FP8X4), w3_sc[:, a, cols]
 
-        ring = [0]
-
-        def next_bank(name):
-            ring[0] = ring[0] + 1
-            return bank((ring[0] - 1) % 3, [P, HALF], name)
+        def product_bank(which, c, h):
+            u = 2 * c + h
+            i = {"a": u % 2, "b": 2 + u % 3, "e": 5 + u % 3}[which]
+            return bank(i, [P, HALF], "%s_%d" % (which, u))
 
         def product_rows(which, c, h):
-            acc = next_bank("%s_%d_%d" % (which, c, h))
+            acc = product_bank(which, c, h)
             for a in range(2):
                 w, ws = w_operand(which, a, c)
                 v, vs = v_operand(which, a, h, 0, HALF)
@@ -193,7 +190,7 @@ def tile_list_address_repair_page_kernel(
             return acc
 
         def product_turned(which, c, h):
-            acc = next_bank("%sT_%d_%d" % (which, c, h))
+            acc = product_bank(which, c, h)
             for jb in range(4):
                 for a in range(2):
                     w, ws = w_operand(which, a, c)
@@ -215,86 +212,92 @@ def tile_list_address_repair_page_kernel(
         def blocks(t):
             return [t[:, P * b : P * (b + 1)] for b in range(4)]
 
-        def work(name, u):
-            return sbuf([P, HALF], F32, "%s%d" % (name, u), tag=name, bufs=2)
-
-
-        def spread_3v(u, res):
-            c, h = divmod(u, 2)
-            pa = product_rows("a", c, h)
-            pe = product_rows("e", c, h)
-            pb = product_rows("b", c, h)
-            a_sb, hi = work("ta", u), work("tb", u)
-            lo = sbuf([P, HALF], F32, "lo%d" % u, tag="held%d" % u)
-            nc.scalar.copy(a_sb[:], pa[:])
-            nc.vector.tensor_tensor(lo[:], pe[:], a_sb[:], ALU.min)
-            nc.vector.tensor_tensor(hi[:], pb[:], a_sb[:], ALU.max)
-            nc.vector.tensor_tensor(res, lo[:], hi[:], ALU.subtract)
-
-        def spread_1v(u, res):
-            c, h = divmod(u, 2)
-            na, e_sb, b_sb = work("ta", u), work("te", u), work("tb", u)
-            pa = product_turned("a", c, h)
-            nc.scalar.activation(na[:], pa[:], ACT.Copy, scale=-1.0)
-            pb = product_turned("b", c, h)
-            nc.scalar.copy(b_sb[:], pb[:])
-            pe = product_turned("e", c, h)
-            nc.scalar.copy(e_sb[:], pe[:])
-            d1 = bank(3, [P, HALF], "d1_%d" % u)
-            turn_and_add(d1, [blocks(na), blocks(b_sb)])
-            d2 = bank(4 + u % 4, [P, HALF], "d2_%d" % u)
-            turn_and_add(d2, [blocks(na), blocks(e_sb)])
-            r1 = sbuf([P, HALF], F32, "r1_%d" % u, tag="held%d" % u)
-            nc.scalar.activation(r1[:], d1[:], ACT.Relu)
-            nc.vector.scalar_tensor_tensor(res, d2[:], 0.0, r1[:], ALU.min, ALU.subtract)
+        def work(name, u, tag=None, bufs=1):
+            return sbuf([P, HALF], F32, "%s%d" % (name, u), tag=tag, bufs=bufs)
 
         picked = {}
 
         def pick_first(c, tag):
-            g = sbuf([P, HALF], F32, "g%d" % c, tag=tag)
+            g = work("g", c, tag)
             nc.vector.tensor_copy(g[:], pg0[c][:].indirect(half_of(idx3, 0)))
             picked[(c, 0)] = g[:]
 
-        for c in range(4):
-            if c == 3:
-                neg_h = sbuf([P, 4 * HALF], F32, "h_last", tag="late")
+        def put_state(u, values, factor):
+            c, h = divmod(u, 2)
+            nc.vector.tensor_tensor(pg0[c][:].indirect(half_of(idx2, h)), values, factor, ALU.mult)
+
+        def direct_unit(u):
+            c, h = divmod(u, 2)
+            pa = product_rows("a", c, h)
+            pe = product_rows("e", c, h)
+            pb = product_rows("b", c, h)
+            a_sb, lo, hi = work("a_sb", u, "neg_a", 3), work("lo", u, "lo", 3), work("hi", u, "hi", 3)
+            nc.scalar.copy(a_sb[:], pa[:])
+            nc.vector.tensor_tensor(lo[:], pe[:], a_sb[:], ALU.min)
+            nc.vector.tensor_tensor(hi[:], pb[:], a_sb[:], ALU.max)
+            spread = work("spread", u)
+            nc.vector.tensor_tensor(spread[:], hi[:], lo[:], ALU.subtract)
+            wg = work("wg", u)
+            nc.scalar.activation(wg[:], wgs_t[:, HALF * h : HALF * (h + 1)], ACT.Copy, scale=gain_t[:, c : c + 1])
+            put_state(u, spread[:], wg[:])
+
+        neg_a, extremes = {}, {}
+
+        def turned_a(u):
+            c, h = divmod(u, 2)
+            pa = product_turned("a", c, h)
+            neg_a[u] = work("neg_a", u, "neg_a7", 1) if u == 7 else work("neg_a", u, "neg_a", 3)
+            nc.scalar.activation(neg_a[u][:], pa[:], ACT.Copy, scale=-1.0)
+
+        def turned_extremes(u):
+            c, h = divmod(u, 2)
+            pb = product_turned("b", c, h)
+            pe = product_turned("e", c, h)
+            hi, neg_lo = work("hi", u, "hi", 3), work("neg_lo", u, "lo", 3)
+            nc.vector.scalar_tensor_tensor(hi[:], neg_a[u][:], -1.0, pb[:], ALU.mult, ALU.max)
+            nc.vector.scalar_tensor_tensor(neg_lo[:], pe[:], -1.0, neg_a[u][:], ALU.mult, ALU.max)
+            extremes[u] = (hi, neg_lo)
+
+        def turned_finish(u):
+            c, h = divmod(u, 2)
+            f = bank(u % 2, [P, HALF], "f%d" % u)
+            turn_and_add(f, [blocks(t) for t in extremes[u]])
+            if u == 7:
+                res = work("h", u, "late")[:]
             else:
-                neg_h = sbuf([P, S], F32, "h%d" % c, tag="h", bufs=2)
-            for h in range(2):
-                u = 2 * c + h
-                cols = slice(HALF * h, HALF * (h + 1))
-                if PATHS[u] == "3V":
-                    spread_3v(u, neg_h[:, cols])
-                else:
-                    spread_1v(u, neg_h[:, cols])
-                if c == 1:
-                    w1_q[u] = quantize_w1(u)
-                if c < WHOLE:
-                    if u == 0:
-                        wg = sbuf([P, HALF], F32, "wg_first")
-                    else:
-                        wg = sbuf([P, HALF], F32, "wg_half%d" % u)
-                    nc.scalar.activation(wg[:], wgs_t[:, cols], ACT.Copy, scale=neg_gain[:, c : c + 1])
-                    if h == 0 and c > 0:
-                        pick_first(c - 1, None)
-                    nc.vector.tensor_tensor(pg0[c][:].indirect(half_of(idx2, h)), neg_h[:, cols], wg[:], ALU.mult)
-                    if u == 0:
-                        w1_q[1] = quantize_w1(1)
-            if c >= WHOLE:
-                wg = sbuf([P, S], F32, "wg%d" % c)
-                nc.scalar.activation(wg[:], wgs_t[:], ACT.Copy, scale=neg_gain[:, c : c + 1])
-                pick_first(c - 1, "held%d" % (2 * c + 1))
-                nc.vector.tensor_tensor(pg0[c][:].indirect(idx2[:]), neg_h[:, 0:S], wg[:], ALU.mult)
+                res = work("h", u, "h", 3)[:]
+            nc.scalar.activation(res, f[:], ACT.Copy, scale=gain_t[:, c : c + 1])
+            put_state(u, res, wgs_t[:, HALF * h : HALF * (h + 1)])
+
+        direct_unit(0)
+        w1_q[1] = quantize_w1(1, "wg0")
+        direct_unit(1)
+        w1_q[2] = quantize_w1(2, "wg1")
+        w1_q[3] = quantize_w1(3, "spread1")
+        pick_first(0, None)
+        turned_a(2)
+        turned_extremes(2)
+        turned_a(3)
+        for u in range(3, 8):
+            turned_extremes(u)
+            if u < 7:
+                turned_a(u + 1)
+            turned_finish(u - 1)
+            if u == 4:
+                pick_first(1, None)
+        pick_first(2, "neg_a7")
+        turned_finish(7)
         pick_first(3, None)
-        late = sbuf([P, 4 * HALF], F32, "g_late", tag="late")
-        for c in range(4):
+        late = sbuf([P, 3 * HALF], F32, "g_late", tag="late")
+        for c in range(3):
             picked[(c, 1)] = late[:, HALF * c : HALF * (c + 1)]
             nc.vector.tensor_copy(picked[(c, 1)], pg0[c][:].indirect(half_of(idx3, 1)))
 
         w4_raw = sbuf([P, 4, N], F32, "w4_raw", tag="w1_raw2")
         nc.sync.dma_start(w4_raw[:], w4.rearrange("(p j) n -> p j n", j=4))
         idx4 = load_list(offs4, "idx4")
-        wgo_t = [load_half(wgo, h, "wgo%d" % h) for h in range(2)]
+        wgo_t = sbuf([P, NP], F32, "wgo_t")
+        nc.sync.dma_start(wgo_t[:], wgo)
         pg1 = [load_rows(page1, n, "page1_%d" % n, tag="tab%d" % n if n < 2 else None) for n in range(4)]
         w4_bf = sbuf([P, N, 4], BF16, "w4_bf")
         nc.scalar.copy(w4_bf[:], w4_raw[:].rearrange("p j n -> p n j"))
@@ -305,49 +308,56 @@ def tile_list_address_repair_page_kernel(
         nc.scalar.activation(neg_mid[:], mid_t[:], ACT.Copy, scale=-1.0)
         mid_blocks = [neg_mid[:, c : c + 1].to_broadcast([P, P]) for c in range(4)]
 
-        def quantize_x(h, turn_banks, word_banks):
-            xi = sbuf([P, HALF, 2], F32, "xi%d" % h)
-            for pair in range(2):
-                words = bank(word_banks[pair], [P, 2, 2, P], "words%d_%d" % (h, pair))
-                for b in range(2):
-                    jb = 2 * pair + b
-                    xt = bank(turn_banks[jb], [P, H], "xt%d_%d" % (h, jb))
-                    turn_and_add(xt, [mid_blocks, [picked[(c, h)][:, P * jb : P * (jb + 1)] for c in range(4)]])
-                    xb = sbuf([P, 2, P, 2], BF16, "xb%d_%d" % (h, jb), tag="xb", bufs=4)
-                    nc.scalar.copy(xb[:], xt[:].rearrange("j (q u e) -> j u q e", u=2, e=2))
-                    xw = xb[:].rearrange("j u q e -> j (u q e)").bitcast(F32)
-                    for u in range(2):
-                        nc.tensor.transpose(words[:, b, u, :], xw[:, P * u : P * (u + 1)], ident[:])
-                nc.scalar.copy(
-                    xi[:, 2 * P * pair : 2 * P * (pair + 1), :].rearrange("p (b j) u -> p b j u", b=2),
-                    words[:].rearrange("p b u j -> p b j u"),
-                )
-            codes = sbuf([P, HALF], U32, "x_q%d" % h)
-            scales = sbuf([P, HALF], U8, "x_s%d" % h)
-            nc.vector.quantize_mx(
-                out=codes[:].bitcast(FP8X4), scales=scales[:],
-                in_=xi[:].rearrange("p j u -> p (j u)").bitcast(BF16),
-            )
-            return codes, scales
+        def interleave_x(h, pair, turn_banks, word_bank, xi):
+            words = bank(word_bank, [P, 2, 2, P], "words%d_%d" % (h, pair))
+            for b in range(2):
+                jb = 2 * pair + b
+                xt = bank(turn_banks[b], [P, H], "xt%d_%d" % (h, jb))
+                turn_and_add(xt, [mid_blocks, [picked[(c, h)][:, P * jb : P * (jb + 1)] for c in range(4)]])
+                xb = sbuf([P, 2, P, 2], BF16, "xb%d_%d" % (h, jb), tag="xb", bufs=4)
+                nc.scalar.copy(xb[:], xt[:].rearrange("j (q u e) -> j u q e", u=2, e=2))
+                xw = xb[:].rearrange("j u q e -> j (u q e)").bitcast(F32)
+                for u in range(2):
+                    nc.tensor.transpose(words[:, b, u, :], xw[:, P * u : P * (u + 1)], ident[:])
+            nc.scalar.copy(xi.rearrange("p (b j u) -> p b j u", b=2, u=2), words[:].rearrange("p b u j -> p b j u"))
 
-        def put_result(n, h, x_q, y_bank):
-            y = bank(y_bank, [P, HALF], "y%d_%d" % (n, h))
+        x_q = sbuf([P, NP], U32, "x_q")
+        x_s = sbuf([P, NP], U8, "x_s")
+
+        def quantize_x(j0, j1, xi):
+            nc.vector.quantize_mx(out=x_q[:, j0:j1].bitcast(FP8X4), scales=x_s[:, j0:j1], in_=xi.bitcast(BF16))
+
+        def put_result(n, j0, j1, y_bank):
+            y = bank(y_bank, [P, j1 - j0], "y%d_%d" % (n, j0))
             cols = slice(P * n, P * (n + 1))
             nc.tensor.matmul_mx(
                 out=y[:], lhsT=w4_q[:, cols].bitcast(FP8X4), lhsT_scale=w4_s[:, cols],
-                rhs=x_q[0][:].bitcast(FP8X4), rhs_scale=x_q[1][:], start=True, stop=True,
+                rhs=x_q[:, j0:j1].bitcast(FP8X4), rhs_scale=x_s[:, j0:j1], start=True, stop=True,
             )
-            act = sbuf([P, HALF], F32, "act%d_%d" % (n, h), tag="act", bufs=3)
+            act = sbuf([P, j1 - j0], F32, "act%d_%d" % (n, j0), tag="act", bufs=6)
             nc.scalar.activation(act[:], y[:], ACT.Gelu_apprx_tanh)
-            nc.vector.tensor_tensor(pg1[n][:].indirect(half_of(idx4, h)), act[:], wgo_t[h][:], ALU.mult)
-            if h == 1:
+            nc.vector.tensor_tensor(pg1[n][:].indirect(idx4[:, j0 // 16 : j1 // 16]), act[:], wgo_t[:, j0:j1], ALU.mult)
+            if j1 == NP:
                 nc.sync.dma_start(out[P * n : P * (n + 1), :], pg1[n][:])
 
-        x0 = quantize_x(0, (0, 1, 2, 3), (4, 5))
-        put_result(0, 0, x0, 6)
-        put_result(1, 0, x0, 7)
-        x1 = quantize_x(1, (6, 7, 6, 7), (4, 5))
-        put_result(2, 0, x0, 4)
-        put_result(3, 0, x0, 5)
+        xi0 = work("xi", 0)
+        interleave_x(0, 0, (4, 7), 3, xi0[:])
+        quantize_x(0, 256, xi0[:])
+        g_last = work("g_last", 0, "xi0")
+        picked[(3, 1)] = g_last[:]
+        nc.vector.tensor_copy(g_last[:], pg0[3][:].indirect(half_of(idx3, 1)))
+        xi1 = work("xi", 1)
+        interleave_x(0, 1, (2, 5), 6, xi1[:])
+        put_result(0, 0, 256, 0)
+        quantize_x(256, 512, xi1[:])
+        put_result(1, 0, 256, 1)
+        put_result(0, 256, 512, 4)
+        put_result(1, 256, 512, 7)
+        put_result(2, 0, 512, 0)
+        xi2 = sbuf([P, 2 * HALF], F32, "xi2")
+        interleave_x(1, 0, (0, 7), 3, xi2[:, 0:HALF])
+        interleave_x(1, 1, (0, 7), 6, xi2[:, HALF : 2 * HALF])
+        quantize_x(512, 1024, xi2[:])
+        put_result(3, 0, 512, 6)
         for n in range(4):
-            put_result(n, 1, x1, n)
+            put_result(n, 512, 1024, (2, 4, 5, 1)[n])

@@ -33,8 +33,8 @@ def tile_list_address_repair_page_kernel(
         sb = ctx.enter_context(tc.tile_pool(name="sb", bufs=1))
         psum = ctx.enter_context(tc.psum_pool(name="psum", bufs=1))
 
-        def sbuf(shape, dtype, name, tag=None, bufs=1):
-            return sb.tile(shape, dtype, name=name, tag=tag or name, bufs=bufs, align_bytes=64)
+        def sbuf(shape, dtype, name, tag=None, bufs=1, pool=sb):
+            return pool.tile(shape, dtype, name=name, tag=tag or name, bufs=bufs, align_bytes=64)
 
         def bank(i, shape, name):
             return psum.tile(shape, F32, name=name, tag="bank%d" % i)
@@ -47,93 +47,93 @@ def tile_list_address_repair_page_kernel(
         def half_of(lst, h):
             return lst[:, 32 * h : 32 * h + 32]
 
-        tab_sc = sbuf([P, T], U8, "tab_sc")
-        nc.vector.memset(tab_sc[:].bitcast(I32), 0)
-        w3_sc = sbuf([P, 2, H], U8, "w3_sc")
-        nc.vector.memset(w3_sc[:].rearrange("p a n -> p (a n)").bitcast(I32), 0)
-        w2_sc = sbuf([P, 2, H], U8, "w2_sc")
-        nc.gpsimd.memset(w2_sc[:].rearrange("p a n -> p (a n)").bitcast(I32), 0)
-        v_sc1 = sbuf([P, S], U8, "v_sc1")
-        nc.vector.memset(v_sc1[:].bitcast(I32), 0)
-        warm = sbuf([P, 2], F32, "warm")
-        nc.vector.memset(warm[:, 0:1], 0.0)
-        nc.scalar.activation(warm[:, 1:2], warm[:, 0:1], ACT.Gelu_apprx_tanh)
+        with tc.tile_pool(name="early", bufs=1) as early:
+            tab_sc = sbuf([P, T], U8, "tab_sc", pool=early)
+            nc.vector.memset(tab_sc[:].bitcast(I32), 0)
+            w3_sc = sbuf([P, 2, H], U8, "w3_sc")
+            nc.vector.memset(w3_sc[:].rearrange("p a n -> p (a n)").bitcast(I32), 0)
+            w2_sc = sbuf([P, 2, H], U8, "w2_sc")
+            nc.gpsimd.memset(w2_sc[:].rearrange("p a n -> p (a n)").bitcast(I32), 0)
+            v_sc1 = sbuf([P, S], U8, "v_sc1")
+            nc.vector.memset(v_sc1[:].bitcast(I32), 0)
+            warm = sbuf([P, 2], F32, "warm")
+            nc.vector.memset(warm[:, 0:1], 0.0)
+            nc.scalar.activation(warm[:, 1:2], warm[:, 0:1], ACT.Gelu_apprx_tanh)
 
-        ident = sbuf([P, P], F32, "ident")
-        make_identity(nc, ident[:])
+            ident = sbuf([P, P], F32, "ident")
+            make_identity(nc, ident[:])
 
-        def load_w1(c0, c1, tag):
-            t = sbuf([P, 2, 4, P * (c1 - c0)], F32, "w1_raw%d" % c0, tag=tag)
-            for a in range(2):
-                rows = w1[512 * a : 512 * (a + 1), P * c0 : P * c1]
-                nc.sync.dma_start(t[:, a, :, :], rows.rearrange("(p j) c -> p j c", j=4))
-            return t
+            def load_w1(c0, c1, pool):
+                t = sbuf([P, 2, 4, P * (c1 - c0)], F32, "w1_raw%d" % c0, pool=pool)
+                for a in range(2):
+                    rows = w1[512 * a : 512 * (a + 1), P * c0 : P * c1]
+                    nc.sync.dma_start(t[:, a, :, :], rows.rearrange("(p j) c -> p j c", j=4))
+                return t
 
-        def load_w23(c0, c1):
-            t2 = sbuf([P, 2, 2 * P * (c1 - c0)], U8, "w2_w%d" % c0)
-            src2 = w2_words.rearrange("a p n -> p a n")[:, :, 2 * P * c0 : 2 * P * c1]
-            nc.sync.dma_start(t2[:].bitcast(I32), src2.bitcast(I32))
-            t3 = sbuf([P, 2, P * (c1 - c0)], U32, "w3_w%d" % c0)
-            src3 = w3_words.rearrange("a p n t -> p a (n t)")[:, :, 4 * P * c0 : 4 * P * c1]
-            nc.sync.dma_start(t3[:].bitcast(I32), src3.bitcast(I32))
-            return t2, t3
+            def load_w23(c0, c1, pool):
+                t2 = sbuf([P, 2, 2 * P * (c1 - c0)], U8, "w2_w%d" % c0, pool=pool)
+                src2 = w2_words.rearrange("a p n -> p a n")[:, :, 2 * P * c0 : 2 * P * c1]
+                nc.sync.dma_start(t2[:].bitcast(I32), src2.bitcast(I32))
+                t3 = sbuf([P, 2, P * (c1 - c0)], U32, "w3_w%d" % c0, pool=pool)
+                src3 = w3_words.rearrange("a p n t -> p a (n t)")[:, :, 4 * P * c0 : 4 * P * c1]
+                nc.sync.dma_start(t3[:].bitcast(I32), src3.bitcast(I32))
+                return t2, t3
 
-        def load_tab(a):
-            t = sbuf([P, T], U32, "tab_w%d" % a, tag="tab%d" % a)
-            nc.sync.dma_start(t[:].bitcast(I32), tab_words[a].rearrange("p t i -> p (t i)").bitcast(I32))
-            return t
+            def load_tab(a):
+                t = sbuf([P, T], U32, "tab_w%d" % a, tag="tab%d" % a)
+                nc.sync.dma_start(t[:].bitcast(I32), tab_words[a].rearrange("p t i -> p (t i)").bitcast(I32))
+                return t
 
-        def load_rows(src, c, name, tag=None):
-            t = sbuf([P, T2], F32, name, tag=tag)
-            nc.sync.dma_start(t[:], src[P * c : P * (c + 1), :])
-            return t
+            def load_rows(src, c, name, pool, tag=None):
+                t = sbuf([P, T2], F32, name, tag=tag, pool=pool)
+                nc.sync.dma_start(t[:], src[P * c : P * (c + 1), :])
+                return t
 
-        def load_column(vec, name):
-            t = sbuf([P, 4], F32, name)
-            with nc.allow_non_contiguous_dma(reason="one value a partition"):
-                nc.sync.dma_start(t[:], vec.rearrange("(c p) -> p c", p=P))
-            return t
-
-        def load_half(src, h, name):
-            t = sbuf([P, HALF], F32, name)
-            nc.sync.dma_start(t[:], src[:, HALF * h : HALF * (h + 1)])
-            return t
-
-        idx = load_list(offs, "idx")
-        w1_raw0 = load_w1(0, 1, "w1_raw0")
-        for q in (0, 2, 1, 3):
-            nc.sync.dma_start(
-                tab_sc[32 * q : 32 * q + 8, :].bitcast(I32), tab_scales[:, 4 * q : 4 * q + 4, :].bitcast(I32)
-            )
-        tab0 = load_tab(0)
-        for plane, src, queue in ((w3_sc, w3_scales, nc.sync), (w2_sc, w2_scales, nc.gpsimd)):
-            for q in range(4):
-                queue.dma_start(
-                    plane[32 * q : 32 * q + 4, :, :].bitcast(I32),
-                    src[:, 4 * q : 4 * q + 4, :].rearrange("a r n -> r a n").bitcast(I32),
+            idx = load_list(offs, "idx")
+            w1_raw0 = load_w1(0, 1, sb)
+            for q in (0, 2, 1, 3):
+                nc.sync.dma_start(
+                    tab_sc[32 * q : 32 * q + 8, :].bitcast(I32), tab_scales[:, 4 * q : 4 * q + 4, :].bitcast(I32)
                 )
-        w2_0, w3_0 = load_w23(0, 1)
-        tab1 = load_tab(1)
-        v_sc = sbuf([P, S], U8, "v_sc")
-        nc.vector.tensor_copy(v_sc[:], tab_sc[:].indirect(idx[:]))
+            tab0 = load_tab(0)
+            for plane, src, queue in ((w3_sc, w3_scales, nc.sync), (w2_sc, w2_scales, nc.gpsimd)):
+                for q in range(4):
+                    queue.dma_start(
+                        plane[32 * q : 32 * q + 4, :, :].bitcast(I32),
+                        src[:, 4 * q : 4 * q + 4, :].rearrange("a r n -> r a n").bitcast(I32),
+                    )
+            w2_0, w3_0 = load_w23(0, 1, sb)
+            tab1 = load_tab(1)
+            v_sc = sbuf([P, S], U8, "v_sc")
+            nc.vector.tensor_copy(v_sc[:], tab_sc[:].indirect(idx[:]))
+        later = ctx.enter_context(tc.tile_pool(name="later", bufs=1))
         for q in range(4):
             nc.sync.dma_start(
                 v_sc1[32 * q : 32 * q + 4, :].bitcast(I32), v_sc[32 * q + 4 : 32 * q + 8, :].bitcast(I32)
             )
-        wgs_t = sbuf([P, S], F32, "wgs_t")
+        gain_rows = sbuf([P, P], F32, "gain_rows", pool=later)
+        nc.vector.memset(gain_rows[:], 0.0)
+        nc.sync.dma_start(gain_rows[0:4, :], gain.rearrange("(c p) -> c p", p=P))
+        nc.sync.dma_start(gain_rows[4:8, :], mid.rearrange("(c p) -> c p", p=P))
+        wgs_t = sbuf([P, S], F32, "wgs_t", pool=later)
         nc.sync.dma_start(wgs_t[:, 0:HALF], wgs[:, 0:HALF])
-        pg0 = [load_rows(page0, 0, "page0_0")]
-        gain_t = load_column(gain, "gain_t")
+        pg0 = [load_rows(page0, 0, "page0_0", later)]
         idx2 = load_list(offs2, "idx2")
-        w1_raw1 = load_w1(1, 2, "w1_raw1")
-        w2_r, w3_r = load_w23(1, 4)
+        w1_raw1 = load_w1(1, 2, later)
         nc.sync.dma_start(wgs_t[:, HALF:S], wgs[:, HALF:S])
+        w2_r, w3_r = load_w23(1, 4, later)
+        w1_raw2 = load_w1(2, 4, later)
         idx3 = load_list(offs3, "idx3")
-        pg0.append(load_rows(page0, 1, "page0_1"))
-        w1_raw2 = load_w1(2, 4, "w1_raw2")
-        pg0.append(load_rows(page0, 2, "page0_2"))
-        mid_t = load_column(mid, "mid_t")
-        pg0.append(load_rows(page0, 3, "page0_3"))
+        for c in range(1, 4):
+            pg0.append(load_rows(page0, c, "page0_%d" % c, later))
+
+        gain_turned = bank(7, [P, P], "gain_turned")
+        nc.tensor.transpose(gain_turned[:], gain_rows[:], ident[:])
+        gain_t = sbuf([P, 4], F32, "gain_t")
+        nc.scalar.copy(gain_t[:], gain_turned[:, 0:4])
+        negated = sbuf([P, 8], F32, "negated")
+        nc.scalar.activation(negated[:], gain_turned[:, 0:8], ACT.Copy, scale=-1.0)
+        neg_gain, neg_mid = negated[:, 0:4], negated[:, 4:8]
 
 
         def quantize_w1(c, tag):
@@ -181,13 +181,11 @@ def tile_list_address_repair_page_kernel(
             i = {"a": u % 2, "b": 2 + u % 3, "e": 5 + u % 3}[which]
             return bank(i, [P, HALF], "%s_%d" % (which, u))
 
-        def product_rows(which, c, h):
-            acc = product_bank(which, c, h)
+        def product_rows(acc, which, c, h, part):
             for a in range(2):
                 w, ws = w_operand(which, a, c)
-                v, vs = v_operand(which, a, h, 0, HALF)
+                v, vs = v_operand(which, a, h, part.start, part.stop)
                 nc.tensor.matmul_mx(out=acc[:], lhsT=w, lhsT_scale=ws, rhs=v, rhs_scale=vs, start=a == 0, stop=a == 1)
-            return acc
 
         def product_turned(which, c, h):
             acc = product_bank(which, c, h)
@@ -226,17 +224,25 @@ def tile_list_address_repair_page_kernel(
             c, h = divmod(u, 2)
             nc.vector.tensor_tensor(pg0[c][:].indirect(half_of(idx2, h)), values, factor, ALU.mult)
 
-        def direct_unit(u):
+        def direct_unit(u, a_banks):
             c, h = divmod(u, 2)
-            pa = product_rows("a", c, h)
-            pe = product_rows("e", c, h)
-            pb = product_rows("b", c, h)
+            width = HALF // len(a_banks)
+            parts = [slice(width * i, width * (i + 1)) for i in range(len(a_banks))]
             a_sb, lo, hi = work("a_sb", u, "neg_a", 3), work("lo", u, "lo", 3), work("hi", u, "hi", 3)
-            nc.scalar.copy(a_sb[:], pa[:])
-            nc.vector.tensor_tensor(lo[:], pe[:], a_sb[:], ALU.min)
-            nc.vector.tensor_tensor(hi[:], pb[:], a_sb[:], ALU.max)
+            for i, part in zip(a_banks, parts):
+                pa = bank(i, [P, width], "a_%d_%d" % (u, i))
+                product_rows(pa, "a", c, h, part)
+                nc.scalar.copy(a_sb[:, part], pa[:])
+            pe, pb = product_bank("e", c, h), product_bank("b", c, h)
+            product_rows(pe, "e", c, h, slice(0, HALF))
+            product_rows(pb, "b", c, h, slice(0, HALF))
             spread = work("spread", u)
-            nc.vector.tensor_tensor(spread[:], hi[:], lo[:], ALU.subtract)
+            for part in parts:
+                nc.vector.tensor_tensor(lo[:, part], pe[:, part], a_sb[:, part], ALU.min)
+            for part in parts:
+                nc.vector.tensor_tensor(hi[:, part], pb[:, part], a_sb[:, part], ALU.max)
+            for part in parts:
+                nc.vector.tensor_tensor(spread[:, part], hi[:, part], lo[:, part], ALU.subtract)
             wg = work("wg", u)
             nc.scalar.activation(wg[:], wgs_t[:, HALF * h : HALF * (h + 1)], ACT.Copy, scale=gain_t[:, c : c + 1])
             put_state(u, spread[:], wg[:])
@@ -246,7 +252,7 @@ def tile_list_address_repair_page_kernel(
         def turned_a(u):
             c, h = divmod(u, 2)
             pa = product_turned("a", c, h)
-            neg_a[u] = work("neg_a", u, "neg_a7", 1) if u == 7 else work("neg_a", u, "neg_a", 3)
+            neg_a[u] = work("neg_a", u, "neg_a", 3)
             nc.scalar.activation(neg_a[u][:], pa[:], ACT.Copy, scale=-1.0)
 
         def turned_extremes(u):
@@ -258,54 +264,81 @@ def tile_list_address_repair_page_kernel(
             nc.vector.scalar_tensor_tensor(neg_lo[:], pe[:], -1.0, neg_a[u][:], ALU.mult, ALU.max)
             extremes[u] = (hi, neg_lo)
 
+        minus_spread = {}
+
+        def turned_differences(u):
+            c, h = divmod(u, 2)
+            pb = product_turned("b", c, h)
+            b_sb = work("b_sb", u, "hi", 3)
+            nc.scalar.copy(b_sb[:], pb[:])
+            pe = product_turned("e", c, h)
+            e_sb = work("e_sb", u)
+            nc.scalar.copy(e_sb[:], pe[:])
+            d1 = bank(2 + u % 3, [P, HALF], "d1_%d" % u)
+            turn_and_add(d1, [blocks(neg_a[u]), blocks(b_sb)])
+            d2 = bank(5 + u % 3, [P, HALF], "d2_%d" % u)
+            turn_and_add(d2, [blocks(neg_a[u]), blocks(e_sb)])
+            r1 = work("r1_", u, "r1_7", 1) if u == 7 else work("r1_", u, "lo", 3)
+            nc.scalar.activation(r1[:], d1[:], ACT.Relu)
+            minus_spread[u] = work("h", u, "late") if u == 7 else work("h", u, "h", 3)
+            nc.vector.scalar_tensor_tensor(minus_spread[u][:], d2[:], 0.0, r1[:], ALU.min, ALU.subtract)
+
+        def differences_finish(u):
+            c, h = divmod(u, 2)
+            wg = work("wg", u, "e_sb%d" % (u + 1))
+            nc.scalar.activation(wg[:], wgs_t[:, HALF * h : HALF * (h + 1)], ACT.Copy, scale=neg_gain[:, c : c + 1])
+            put_state(u, minus_spread[u][:], wg[:])
+
         def turned_finish(u):
             c, h = divmod(u, 2)
             f = bank(u % 2, [P, HALF], "f%d" % u)
             turn_and_add(f, [blocks(t) for t in extremes[u]])
-            if u == 7:
-                res = work("h", u, "late")[:]
-            else:
-                res = work("h", u, "h", 3)[:]
+            res = work("h", u, "h", 3)[:]
             nc.scalar.activation(res, f[:], ACT.Copy, scale=gain_t[:, c : c + 1])
             put_state(u, res, wgs_t[:, HALF * h : HALF * (h + 1)])
 
-        direct_unit(0)
+        direct_unit(0, (0, 4))
         w1_q[1] = quantize_w1(1, "wg0")
-        direct_unit(1)
+        direct_unit(1, (1,))
         w1_q[2] = quantize_w1(2, "wg1")
-        w1_q[3] = quantize_w1(3, "spread1")
         pick_first(0, None)
         turned_a(2)
         turned_extremes(2)
         turned_a(3)
-        for u in range(3, 8):
-            turned_extremes(u)
+        turned_extremes(3)
+        turned_a(4)
+        turned_finish(2)
+        turned_differences(4)
+        w1_q[3] = quantize_w1(3, "e_sb4")
+        turned_a(5)
+        turned_finish(3)
+        pick_first(1, None)
+        for u in range(5, 8):
+            turned_differences(u)
             if u < 7:
                 turned_a(u + 1)
-            turned_finish(u - 1)
-            if u == 4:
-                pick_first(1, None)
-        pick_first(2, "neg_a7")
-        turned_finish(7)
+            differences_finish(u - 1)
+        pick_first(2, "r1_7")
+        differences_finish(7)
         pick_first(3, None)
         late = sbuf([P, 3 * HALF], F32, "g_late", tag="late")
         for c in range(3):
             picked[(c, 1)] = late[:, HALF * c : HALF * (c + 1)]
             nc.vector.tensor_copy(picked[(c, 1)], pg0[c][:].indirect(half_of(idx3, 1)))
 
-        w4_raw = sbuf([P, 4, N], F32, "w4_raw", tag="w1_raw2")
+        w4_raw = sbuf([P, 4, N], F32, "w4_raw", tag="w1_raw2", pool=later)
         nc.sync.dma_start(w4_raw[:], w4.rearrange("(p j) n -> p j n", j=4))
         idx4 = load_list(offs4, "idx4")
-        wgo_t = sbuf([P, NP], F32, "wgo_t")
+        wgo_t = sbuf([P, NP], F32, "wgo_t", pool=later)
         nc.sync.dma_start(wgo_t[:], wgo)
-        pg1 = [load_rows(page1, n, "page1_%d" % n, tag="tab%d" % n if n < 2 else None) for n in range(4)]
-        w4_bf = sbuf([P, N, 4], BF16, "w4_bf")
-        nc.scalar.copy(w4_bf[:], w4_raw[:].rearrange("p j n -> p n j"))
+        pg1 = [load_rows(page1, n, "page1_%d" % n, sb, "tab%d" % n) for n in range(2)]
+        pg1.extend([load_rows(page1, n, "page1_%d" % n, later) for n in range(2, 4)])
+        w4_bf = sbuf([P, N, 4], BF16, "w4_bf", tag="e_sb4")
+        for n0 in (0, N // 2):
+            nc.scalar.copy(w4_bf[:, n0 : n0 + N // 2, :], w4_raw[:, :, n0 : n0 + N // 2].rearrange("p j n -> p n j"))
         w4_q = sbuf([P, N], U32, "w4_q")
         w4_s = sbuf([P, N], U8, "w4_s")
         nc.vector.quantize_mx(out=w4_q[:].bitcast(FP8X4), scales=w4_s[:], in_=w4_bf[:].rearrange("p n j -> p (n j)"))
-        neg_mid = sbuf([P, 4], F32, "neg_mid")
-        nc.scalar.activation(neg_mid[:], mid_t[:], ACT.Copy, scale=-1.0)
         mid_blocks = [neg_mid[:, c : c + 1].to_broadcast([P, P]) for c in range(4)]
 
         def interleave_x(h, pair, turn_banks, word_bank, xi):
@@ -355,9 +388,9 @@ def tile_list_address_repair_page_kernel(
         put_result(1, 256, 512, 7)
         put_result(2, 0, 512, 0)
         xi2 = sbuf([P, 2 * HALF], F32, "xi2")
-        interleave_x(1, 0, (0, 7), 3, xi2[:, 0:HALF])
-        interleave_x(1, 1, (0, 7), 6, xi2[:, HALF : 2 * HALF])
+        interleave_x(1, 0, (2, 5), 3, xi2[:, 0:HALF])
+        interleave_x(1, 1, (4, 7), 6, xi2[:, HALF : 2 * HALF])
         quantize_x(512, 1024, xi2[:])
         put_result(3, 0, 512, 6)
         for n in range(4):
-            put_result(n, 512, 1024, (2, 4, 5, 1)[n])
+            put_result(n, 512, 1024, (1, 0, 2, 5)[n])

from contextlib import ExitStack

import concourse.mybir as mybir
from concourse.masks import make_identity

K, T, S, H, T2, NP, N = 1024, 4096, 1024, 512, 2048, 1024, 512
FLOPS = 3 * 2 * K * H * S + 2 * H * N * NP

F32 = mybir.dt.float32
BF16 = mybir.dt.bfloat16
I32 = mybir.dt.int32
U32 = mybir.dt.uint32
U16 = mybir.dt.uint16
U8 = mybir.dt.uint8
FP8X4 = mybir.dt.float8_e4m3fn_x4
FP4X4 = mybir.dt.float4_e2m1fn_x4
ALU = mybir.AluOpType
ACT = mybir.ActivationFunctionType

P = 128
HALF = 512
WHOLE = 2
PATHS = ["3V","1V","1V","1V","1V","1V","1V","1V"]


def tile_list_address_repair_page_kernel(
    tc, tab_words, tab_scales, offs, w1, w2_words, w2_scales, w3_words, w3_scales, gain,
    page0, wgs, offs2, offs3, mid, w4, page1, wgo, offs4, out,
):
    nc = tc.nc
    with ExitStack() as ctx:
        lists = ctx.enter_context(tc.tile_pool(name="lists", bufs=1))
        sb = ctx.enter_context(tc.tile_pool(name="sb", bufs=1))
        psum = ctx.enter_context(tc.psum_pool(name="psum", bufs=1))

        def sbuf(shape, dtype, name, tag=None, bufs=1, pool=sb):
            return pool.tile(shape, dtype, name=name, tag=tag or name, bufs=bufs, align_bytes=64)

        def bank(i, shape, name):
            return psum.tile(shape, F32, name=name, tag="bank%d" % i)

        def load_list(src, name):
            t = lists.tile([P, 64], U16, name=name)
            nc.sync.dma_start(t[:], src)
            return t

        def half_of(lst, h):
            return lst[:, 32 * h : 32 * h + 32]

        with tc.tile_pool(name="early", bufs=1) as early:
            tab_sc = sbuf([P, T], U8, "tab_sc", pool=early)
            nc.vector.memset(tab_sc[:].bitcast(I32), 0)
            w3_sc = sbuf([P, 2, H], U8, "w3_sc")
            nc.vector.memset(w3_sc[:].rearrange("p a n -> p (a n)").bitcast(I32), 0)
            w2_sc = sbuf([P, 2, H], U8, "w2_sc")
            nc.gpsimd.memset(w2_sc[:].rearrange("p a n -> p (a n)").bitcast(I32), 0)
            v_sc1 = sbuf([P, S], U8, "v_sc1")
            nc.vector.memset(v_sc1[:].bitcast(I32), 0)
            warm = sbuf([P, 2], F32, "warm")
            nc.vector.memset(warm[:, 0:1], 0.0)
            nc.scalar.activation(warm[:, 1:2], warm[:, 0:1], ACT.Gelu_apprx_tanh)

            ident = sbuf([P, P], F32, "ident")
            make_identity(nc, ident[:])

            def load_w1(c0, c1, pool):
                t = sbuf([P, 2, 4, P * (c1 - c0)], F32, "w1_raw%d" % c0, pool=pool)
                for a in range(2):
                    rows = w1[512 * a : 512 * (a + 1), P * c0 : P * c1]
                    nc.sync.dma_start(t[:, a, :, :], rows.rearrange("(p j) c -> p j c", j=4))
                return t

            def load_w23(c0, c1, pool):
                t2 = sbuf([P, 2, 2 * P * (c1 - c0)], U8, "w2_w%d" % c0, pool=pool)
                src2 = w2_words.rearrange("a p n -> p a n")[:, :, 2 * P * c0 : 2 * P * c1]
                nc.sync.dma_start(t2[:].bitcast(I32), src2.bitcast(I32))
                t3 = sbuf([P, 2, P * (c1 - c0)], U32, "w3_w%d" % c0, pool=pool)
                src3 = w3_words.rearrange("a p n t -> p a (n t)")[:, :, 4 * P * c0 : 4 * P * c1]
                nc.sync.dma_start(t3[:].bitcast(I32), src3.bitcast(I32))
                return t2, t3

            def load_tab(a):
                t = sbuf([P, T], U32, "tab_w%d" % a, tag="tab%d" % a)
                nc.sync.dma_start(t[:].bitcast(I32), tab_words[a].rearrange("p t i -> p (t i)").bitcast(I32))
                return t

            def load_rows(src, c, name, pool, tag=None):
                t = sbuf([P, T2], F32, name, tag=tag, pool=pool)
                nc.sync.dma_start(t[:], src[P * c : P * (c + 1), :])
                return t

            idx = load_list(offs, "idx")
            w1_raw0 = load_w1(0, 1, sb)
            for q in (0, 2, 1, 3):
                nc.sync.dma_start(
                    tab_sc[32 * q : 32 * q + 8, :].bitcast(I32), tab_scales[:, 4 * q : 4 * q + 4, :].bitcast(I32)
                )
            tab0 = load_tab(0)
            for plane, src, queue in ((w3_sc, w3_scales, nc.sync), (w2_sc, w2_scales, nc.gpsimd)):
                for q in range(4):
                    queue.dma_start(
                        plane[32 * q : 32 * q + 4, :, :].bitcast(I32),
                        src[:, 4 * q : 4 * q + 4, :].rearrange("a r n -> r a n").bitcast(I32),
                    )
            w2_0, w3_0 = load_w23(0, 1, sb)
            tab1 = load_tab(1)
            v_sc = sbuf([P, S], U8, "v_sc")
            nc.vector.tensor_copy(v_sc[:], tab_sc[:].indirect(idx[:]))
        later = ctx.enter_context(tc.tile_pool(name="later", bufs=1))
        for q in range(4):
            nc.sync.dma_start(
                v_sc1[32 * q : 32 * q + 4, :].bitcast(I32), v_sc[32 * q + 4 : 32 * q + 8, :].bitcast(I32)
            )
        gain_rows = sbuf([P, P], F32, "gain_rows", pool=later)
        nc.vector.memset(gain_rows[:], 0.0)
        nc.sync.dma_start(gain_rows[0:4, :], gain.rearrange("(c p) -> c p", p=P))
        nc.sync.dma_start(gain_rows[4:8, :], mid.rearrange("(c p) -> c p", p=P))
        wgs_t = sbuf([P, S], F32, "wgs_t", pool=later)
        nc.sync.dma_start(wgs_t[:, 0:HALF], wgs[:, 0:HALF])
        pg0 = [load_rows(page0, 0, "page0_0", later)]
        idx2 = load_list(offs2, "idx2")
        w1_raw1 = load_w1(1, 2, later)
        nc.sync.dma_start(wgs_t[:, HALF:S], wgs[:, HALF:S])
        w2_r, w3_r = load_w23(1, 4, later)
        w1_raw2 = load_w1(2, 4, later)
        idx3 = load_list(offs3, "idx3")
        for c in range(1, 4):
            pg0.append(load_rows(page0, c, "page0_%d" % c, later))

        gain_turned = bank(7, [P, P], "gain_turned")
        nc.tensor.transpose(gain_turned[:], gain_rows[:], ident[:])
        gain_t = sbuf([P, 4], F32, "gain_t")
        nc.scalar.copy(gain_t[:], gain_turned[:, 0:4])
        negated = sbuf([P, 8], F32, "negated")
        nc.scalar.activation(negated[:], gain_turned[:, 0:8], ACT.Copy, scale=-1.0)
        neg_gain, neg_mid = negated[:, 0:4], negated[:, 4:8]


        def quantize_w1(c, tag):
            raw, off = ((w1_raw0, 0), (w1_raw1, 0), (w1_raw2, 0), (w1_raw2, P))[c]
            grouped = sbuf([P, 2, P, 4], BF16, "w1_bf%d" % c, tag="w1_bf", bufs=2)
            nc.scalar.copy(grouped[:], raw[:, :, :, off : off + P].rearrange("p a j c -> p a c j"))
            codes = sbuf([P, 2 * P], U32, "w1_q%d" % c, tag=tag)
            scales = sbuf([P, 2 * P], U8, "w1_s%d" % c)
            nc.vector.quantize_mx(
                out=codes[:].bitcast(FP8X4), scales=scales[:], in_=grouped[:].rearrange("p a c j -> p (a c j)")
            )
            return codes, scales

        w1_q = {0: quantize_w1(0, None)}
        v0 = sbuf([P, S], U32, "v0")
        nc.vector.tensor_copy(v0[:], tab0[:].indirect(idx[:]))
        v1 = []
        for h in range(2):
            t = sbuf([P, HALF], U32, "v1_%d" % h)
            nc.vector.tensor_copy(t[:], tab1[:].indirect(half_of(idx, h)))
            v1.append(t)


        def v_operand(which, a, h, j0, j1):
            cols = slice(HALF * h + j0, HALF * h + j1)
            if a == 0:
                return v0[:, cols].bitcast(FP8X4), v_sc[:, cols]
            plane = v_sc1[:, cols] if which == "b" else v_sc[4:P, cols]
            return v1[h][:, j0:j1].bitcast(FP8X4), plane

        def w_operand(which, a, c):
            cols = slice(P * c, P * (c + 1))
            if which == "a":
                codes, scales = w1_q[c]
                return codes[:, P * a : P * (a + 1)].bitcast(FP8X4), scales[:, P * a : P * (a + 1)]
            k = 0 if c == 0 else c - 1
            if which == "b":
                t = w2_0 if c == 0 else w2_r
                return t[:, a, 2 * P * k : 2 * P * (k + 1)].bitcast(FP4X4), w2_sc[:, a, cols]
            t = w3_0 if c == 0 else w3_r
            return t[:, a, P * k : P * (k + 1)].bitcast(FP8X4), w3_sc[:, a, cols]

        def product_bank(which, c, h):
            u = 2 * c + h
            i = {"a": u % 2, "b": 2 + u % 3, "e": 5 + u % 3}[which]
            return bank(i, [P, HALF], "%s_%d" % (which, u))

        def product_rows(acc, which, c, h, part):
            for a in range(2):
                w, ws = w_operand(which, a, c)
                v, vs = v_operand(which, a, h, part.start, part.stop)
                nc.tensor.matmul_mx(out=acc[:], lhsT=w, lhsT_scale=ws, rhs=v, rhs_scale=vs, start=a == 0, stop=a == 1)

        def product_turned(which, c, h):
            acc = product_bank(which, c, h)
            for jb in range(4):
                for a in range(2):
                    w, ws = w_operand(which, a, c)
                    v, vs = v_operand(which, a, h, P * jb, P * (jb + 1))
                    nc.tensor.matmul_mx(
                        out=acc[:, P * jb : P * (jb + 1)], lhsT=v, lhsT_scale=vs, rhs=w, rhs_scale=ws,
                        start=a == 0, stop=a == 1,
                    )
            return acc

        def turn_and_add(acc, terms):
            steps = [(b, term[b]) for term in terms for b in range(len(term))]
            for i, (b, src) in enumerate(steps):
                nc.tensor.matmul(
                    acc[:, P * b : P * (b + 1)], src, ident[:], is_transpose=True,
                    start=i == 0, stop=i == len(steps) - 1,
                )

        def blocks(t):
            return [t[:, P * b : P * (b + 1)] for b in range(4)]

        def work(name, u, tag=None, bufs=1):
            return sbuf([P, HALF], F32, "%s%d" % (name, u), tag=tag, bufs=bufs)

        picked = {}

        def pick_first(c, tag):
            g = work("g", c, tag)
            nc.vector.tensor_copy(g[:], pg0[c][:].indirect(half_of(idx3, 0)))
            picked[(c, 0)] = g[:]

        def put_state(u, values, factor):
            c, h = divmod(u, 2)
            nc.vector.tensor_tensor(pg0[c][:].indirect(half_of(idx2, h)), values, factor, ALU.mult)

        def direct_unit(u, a_banks):
            c, h = divmod(u, 2)
            width = HALF // len(a_banks)
            parts = [slice(width * i, width * (i + 1)) for i in range(len(a_banks))]
            a_sb, lo, hi = work("a_sb", u, "neg_a", 3), work("lo", u, "lo", 3), work("hi", u, "hi", 3)
            for i, part in zip(a_banks, parts):
                pa = bank(i, [P, width], "a_%d_%d" % (u, i))
                product_rows(pa, "a", c, h, part)
                nc.scalar.copy(a_sb[:, part], pa[:])
            pe, pb = product_bank("e", c, h), product_bank("b", c, h)
            product_rows(pe, "e", c, h, slice(0, HALF))
            product_rows(pb, "b", c, h, slice(0, HALF))
            spread = work("spread", u)
            for part in parts:
                nc.vector.tensor_tensor(lo[:, part], pe[:, part], a_sb[:, part], ALU.min)
            for part in parts:
                nc.vector.tensor_tensor(hi[:, part], pb[:, part], a_sb[:, part], ALU.max)
            for part in parts:
                nc.vector.tensor_tensor(spread[:, part], hi[:, part], lo[:, part], ALU.subtract)
            wg = work("wg", u)
            nc.scalar.activation(wg[:], wgs_t[:, HALF * h : HALF * (h + 1)], ACT.Copy, scale=gain_t[:, c : c + 1])
            put_state(u, spread[:], wg[:])

        neg_a, extremes = {}, {}

        def turned_a(u):
            c, h = divmod(u, 2)
            pa = product_turned("a", c, h)
            neg_a[u] = work("neg_a", u, "neg_a", 3)
            nc.scalar.activation(neg_a[u][:], pa[:], ACT.Copy, scale=-1.0)

        def turned_extremes(u):
            c, h = divmod(u, 2)
            pb = product_turned("b", c, h)
            pe = product_turned("e", c, h)
            hi, neg_lo = work("hi", u, "hi", 3), work("neg_lo", u, "lo", 3)
            nc.vector.scalar_tensor_tensor(hi[:], neg_a[u][:], -1.0, pb[:], ALU.mult, ALU.max)
            nc.vector.scalar_tensor_tensor(neg_lo[:], pe[:], -1.0, neg_a[u][:], ALU.mult, ALU.max)
            extremes[u] = (hi, neg_lo)

        minus_spread = {}

        def turned_differences(u):
            c, h = divmod(u, 2)
            pb = product_turned("b", c, h)
            b_sb = work("b_sb", u, "hi", 3)
            nc.scalar.copy(b_sb[:], pb[:])
            pe = product_turned("e", c, h)
            e_sb = work("e_sb", u)
            nc.scalar.copy(e_sb[:], pe[:])
            d1 = bank(2 + u % 3, [P, HALF], "d1_%d" % u)
            turn_and_add(d1, [blocks(neg_a[u]), blocks(b_sb)])
            d2 = bank(5 + u % 3, [P, HALF], "d2_%d" % u)
            turn_and_add(d2, [blocks(neg_a[u]), blocks(e_sb)])
            r1 = work("r1_", u, "r1_7", 1) if u == 7 else work("r1_", u, "lo", 3)
            nc.scalar.activation(r1[:], d1[:], ACT.Relu)
            minus_spread[u] = work("h", u, "late") if u == 7 else work("h", u, "h", 3)
            nc.vector.scalar_tensor_tensor(minus_spread[u][:], d2[:], 0.0, r1[:], ALU.min, ALU.subtract)

        def differences_finish(u):
            c, h = divmod(u, 2)
            wg = work("wg", u, "e_sb%d" % (u + 1))
            nc.scalar.activation(wg[:], wgs_t[:, HALF * h : HALF * (h + 1)], ACT.Copy, scale=neg_gain[:, c : c + 1])
            put_state(u, minus_spread[u][:], wg[:])

        def turned_finish(u):
            c, h = divmod(u, 2)
            f = bank(u % 2, [P, HALF], "f%d" % u)
            turn_and_add(f, [blocks(t) for t in extremes[u]])
            res = work("h", u, "h", 3)[:]
            nc.scalar.activation(res, f[:], ACT.Copy, scale=gain_t[:, c : c + 1])
            put_state(u, res, wgs_t[:, HALF * h : HALF * (h + 1)])

        direct_unit(0, (0, 4))
        w1_q[1] = quantize_w1(1, "wg0")
        direct_unit(1, (1,))
        w1_q[2] = quantize_w1(2, "wg1")
        pick_first(0, None)
        turned_a(2)
        turned_extremes(2)
        turned_a(3)
        turned_extremes(3)
        turned_a(4)
        turned_finish(2)
        turned_differences(4)
        w1_q[3] = quantize_w1(3, "e_sb4")
        turned_a(5)
        turned_finish(3)
        pick_first(1, None)
        for u in range(5, 8):
            turned_differences(u)
            if u < 7:
                turned_a(u + 1)
            differences_finish(u - 1)
        pick_first(2, "r1_7")
        differences_finish(7)
        pick_first(3, None)
        late = sbuf([P, 3 * HALF], F32, "g_late", tag="late")
        for c in range(3):
            picked[(c, 1)] = late[:, HALF * c : HALF * (c + 1)]
            nc.vector.tensor_copy(picked[(c, 1)], pg0[c][:].indirect(half_of(idx3, 1)))

        w4_raw = sbuf([P, 4, N], F32, "w4_raw", tag="w1_raw2", pool=later)
        nc.sync.dma_start(w4_raw[:], w4.rearrange("(p j) n -> p j n", j=4))
        idx4 = load_list(offs4, "idx4")
        wgo_t = sbuf([P, NP], F32, "wgo_t", pool=later)
        nc.sync.dma_start(wgo_t[:], wgo)
        pg1 = [load_rows(page1, n, "page1_%d" % n, sb, "tab%d" % n) for n in range(2)]
        pg1.extend([load_rows(page1, n, "page1_%d" % n, later) for n in range(2, 4)])
        w4_bf = sbuf([P, N, 4], BF16, "w4_bf", tag="e_sb4")
        for n0 in (0, N // 2):
            nc.scalar.copy(w4_bf[:, n0 : n0 + N // 2, :], w4_raw[:, :, n0 : n0 + N // 2].rearrange("p j n -> p n j"))
        w4_q = sbuf([P, N], U32, "w4_q")
        w4_s = sbuf([P, N], U8, "w4_s")
        nc.vector.quantize_mx(out=w4_q[:].bitcast(FP8X4), scales=w4_s[:], in_=w4_bf[:].rearrange("p n j -> p (n j)"))
        mid_blocks = [neg_mid[:, c : c + 1].to_broadcast([P, P]) for c in range(4)]

        def interleave_x(h, pair, turn_banks, word_bank, xi):
            words = bank(word_bank, [P, 2, 2, P], "words%d_%d" % (h, pair))
            for b in range(2):
                jb = 2 * pair + b
                xt = bank(turn_banks[b], [P, H], "xt%d_%d" % (h, jb))
                turn_and_add(xt, [mid_blocks, [picked[(c, h)][:, P * jb : P * (jb + 1)] for c in range(4)]])
                xb = sbuf([P, 2, P, 2], BF16, "xb%d_%d" % (h, jb), tag="xb", bufs=4)
                nc.scalar.copy(xb[:], xt[:].rearrange("j (q u e) -> j u q e", u=2, e=2))
                xw = xb[:].rearrange("j u q e -> j (u q e)").bitcast(F32)
                for u in range(2):
                    nc.tensor.transpose(words[:, b, u, :], xw[:, P * u : P * (u + 1)], ident[:])
            nc.scalar.copy(xi.rearrange("p (b j u) -> p b j u", b=2, u=2), words[:].rearrange("p b u j -> p b j u"))

        x_q = sbuf([P, NP], U32, "x_q")
        x_s = sbuf([P, NP], U8, "x_s")

        def quantize_x(j0, j1, xi):
            nc.vector.quantize_mx(out=x_q[:, j0:j1].bitcast(FP8X4), scales=x_s[:, j0:j1], in_=xi.bitcast(BF16))

        def put_result(n, j0, j1, y_bank):
            y = bank(y_bank, [P, j1 - j0], "y%d_%d" % (n, j0))
            cols = slice(P * n, P * (n + 1))
            nc.tensor.matmul_mx(
                out=y[:], lhsT=w4_q[:, cols].bitcast(FP8X4), lhsT_scale=w4_s[:, cols],
                rhs=x_q[:, j0:j1].bitcast(FP8X4), rhs_scale=x_s[:, j0:j1], start=True, stop=True,
            )
            act = sbuf([P, j1 - j0], F32, "act%d_%d" % (n, j0), tag="act", bufs=6)
            nc.scalar.activation(act[:], y[:], ACT.Gelu_apprx_tanh)
            nc.vector.tensor_tensor(pg1[n][:].indirect(idx4[:, j0 // 16 : j1 // 16]), act[:], wgo_t[:, j0:j1], ALU.mult)
            if j1 == NP:
                nc.sync.dma_start(out[P * n : P * (n + 1), :], pg1[n][:])

        xi0 = work("xi", 0)
        interleave_x(0, 0, (4, 7), 3, xi0[:])
        quantize_x(0, 256, xi0[:])
        g_last = work("g_last", 0, "xi0")
        picked[(3, 1)] = g_last[:]
        nc.vector.tensor_copy(g_last[:], pg0[3][:].indirect(half_of(idx3, 1)))
        xi1 = work("xi", 1)
        interleave_x(0, 1, (2, 5), 6, xi1[:])
        put_result(0, 0, 256, 0)
        quantize_x(256, 512, xi1[:])
        put_result(1, 0, 256, 1)
        put_result(0, 256, 512, 4)
        put_result(1, 256, 512, 7)
        put_result(2, 0, 512, 0)
        xi2 = sbuf([P, 2 * HALF], F32, "xi2")
        interleave_x(1, 0, (2, 5), 3, xi2[:, 0:HALF])
        interleave_x(1, 1, (4, 7), 6, xi2[:, HALF : 2 * HALF])
        quantize_x(512, 1024, xi2[:])
        put_result(3, 0, 512, 6)
        for n in range(4):
            put_result(n, 512, 1024, (1, 0, 2, 5)[n])
